import numpy as np
import ml_dtypes


def mxq(x, axis, fmt="e4m3"):
    dtype, down = {"e4m3": (ml_dtypes.float8_e4m3fn, 7), "e5m2": (ml_dtypes.float8_e5m2, 14)}[fmt]
    v = np.moveaxis(np.asarray(x, np.float32).astype(ml_dtypes.bfloat16).astype(np.float64), axis, -1)
    blocks = v.reshape(v.shape[:-1] + (-1, 32))
    amax = np.abs(blocks).max(-1, keepdims=True)
    byte = np.maximum(np.where(amax > 0, np.frexp(amax)[1] - 1 + 127, 0) - down, 1)
    scale = np.exp2(byte - 127.0)
    codes = (blocks / scale).astype(np.float32).astype(dtype).astype(np.float64)
    return np.moveaxis((codes * scale).reshape(v.shape), -1, axis)


WIDE = False


def mx_kscale(k):
    if not WIDE:
        return np.ones(k)
    levels = np.array([10, -10, 5, -5, 0])
    if k % 512:
        return np.exp2(np.random.permutation(np.resize(levels, k // 32))).repeat(32)
    a = np.empty((k // 512, 16))
    for p in range(k // 512):
        a[p, :8] = np.random.permutation(np.resize(levels, 8))
        for g in range(8):
            far = levels[np.abs(levels - a[p, g]) >= 10]
            a[p, g + 8] = far[np.random.randint(len(far))]
    return np.exp2(a.ravel()).repeat(32)


def f64(x):
    return np.asarray(x).astype(np.float64)


def striped(idx):
    return np.tile(idx.reshape(-1, 16).T, (8, 1)).astype(np.uint16)


def unstriped(offs):
    return offs[:16].T.reshape(-1).astype(np.int64)


E2M1 = np.array([0.0, 0.5, 1.0, 1.5, 2.0, 3.0, 4.0, 6.0, -0.0, -0.5, -1.0, -1.5, -2.0, -3.0, -4.0, -6.0])


def pack_weight(w, fmt):
    k, n = w.shape
    w = f64(np.asarray(w, np.float32).astype(ml_dtypes.bfloat16)).reshape(k // 32, 32, n)
    amax = np.abs(w).max(1)
    if fmt == "e4m3":
        byte = np.frexp(amax)[1] - 1 + 127 - 7
    else:
        mant, ex = np.frexp(amax / 6.0)
        byte = np.where(mant > 0.5, ex, ex - 1) + 127
    byte = np.clip(np.where(amax > 0, byte, 1), 1, 254)
    scaled = (w * np.exp2(127.0 - byte)[:, None, :]).reshape(k, n).astype(np.float32)
    by_word = np.ascontiguousarray(scaled.reshape(k // 512, 128, 4, n).transpose(0, 1, 3, 2))
    if fmt == "e4m3":
        words = by_word.astype(ml_dtypes.float8_e4m3fn).view(np.uint8)
    else:
        c = by_word.astype(ml_dtypes.float4_e2m1fn).view(np.uint8) & 0xF
        words = (c[..., 0::2] | (c[..., 1::2] << 4)).reshape(k // 512, 128, 2 * n)
    return np.ascontiguousarray(words), np.ascontiguousarray(byte.astype(np.uint8).reshape(k // 512, 16, n))


def unpack_weight(words, scales, fmt):
    g, _, n = scales.shape
    words = np.ascontiguousarray(words).reshape(g, 128, n, -1)
    if fmt == "e4m3":
        vals = words.view(ml_dtypes.float8_e4m3fn).astype(np.float64)
    else:
        nib = np.empty((g, 128, n, 4), np.uint8)
        nib[..., 0::2] = words & 0xF
        nib[..., 1::2] = words >> 4
        vals = E2M1[nib]
    vals = vals * np.repeat(np.exp2(scales.astype(np.float64) - 127.0), 8, axis=1)[..., None]
    return vals.transpose(0, 1, 3, 2).reshape(g * 512, n)


def gelu(v):
    return 0.5 * v * (1.0 + np.tanh(np.sqrt(2.0 / np.pi) * (v + 0.044715 * v**3)))


K, T, S, H, N, T2 = 1024, 4096, 1024, 512, 768, 2048

def setup_inputs():
    n = np.random.standard_normal
    s = mx_kscale(K)[:, None]
    u = mx_kscale(H)[:, None]
    tab_words, tab_scales = pack_weight(n((K, T)) * s, "e4m3")
    w4_words, w4_scales = pack_weight(0.7 * n((K, H)) / np.sqrt(K) / s * u.T, "e2m1")
    w8_words, w8_scales = pack_weight(1.5 * n((H, N)) / np.sqrt(H) / u, "e4m3")
    return {
        "tab_words": tab_words, "tab_scales": tab_scales,
        "offs": striped(np.random.permutation(T)[:S]),
        "offs2": striped(np.random.permutation(T)[:S]),
        "offs3": striped(np.random.permutation(T2)[:S]),
        "wa": (0.55 * n((K, H)) / np.sqrt(K) / s).astype(np.float32),
        "wb": (0.55 * n((K, H)) / np.sqrt(K) / s).astype(np.float32),
        "w4_words": w4_words, "w4_scales": w4_scales,
        "gain": (2.0 * np.exp(0.3 * n(H)) * u[:, 0]).astype(np.float32),
        "w8_words": w8_words, "w8_scales": w8_scales,
        "wind": n((N, S)).astype(np.float32),
        "wgo": np.exp(0.3 * n((128, S))).astype(np.float32),
    }

def reference(tab_words, tab_scales, offs, offs2, offs3, wa, wb, w4_words, w4_scales,
              gain, w8_words, w8_scales, wind, wgo):
    TW = unpack_weight(tab_words, tab_scales, "e4m3")
    v = TW[:, unstriped(offs)]
    v2 = TW[:, unstriped(offs2)]
    climb = np.sin(mxq(f64(wa), 0, "e4m3").T @ v)
    cross = np.cos(mxq(f64(wb), 0, "e4m3").T @ v2)
    own = unpack_weight(w4_words, w4_scales, "e2m1").T @ v
    h = climb * cross * f64(gain)[:, None] + own
    e = unpack_weight(w8_words, w8_scales, "e4m3").T @ mxq(h, 0, "e4m3")
    y = np.tanh(e * f64(wind))
    out = np.zeros((N, T2))
    out[:, unstriped(offs3)] = np.tile(f64(wgo), (N // 128, 1)) * y
    return out

@@ -1,0 +1,259 @@
+import math
+from contextlib import ExitStack
+
+import concourse.mybir as mybir
+from concourse.masks import make_identity
+
+K, T, S, H, N, T2 = 1024, 4096, 1024, 512, 768, 2048
+FLOPS = 2 * (3 * K * H * S + H * N * S)
+
+F32 = mybir.dt.float32
+BF16 = mybir.dt.bfloat16
+I32 = mybir.dt.int32
+U32 = mybir.dt.uint32
+U16 = mybir.dt.uint16
+U8 = mybir.dt.uint8
+FP8X4 = mybir.dt.float8_e4m3fn_x4
+FP4X4 = mybir.dt.float4_e2m1fn_x4
+ALU = mybir.AluOpType
+ACT = mybir.ActivationFunctionType
+
+P = 128
+PACK = 4
+PASSES = K // (P * PACK)
+HALF = 512
+GROUP = 256
+GROUPS = S // GROUP
+BLOCKS = N // P
+EARLY = 4
+ROUNDER = 1.5 * 2**23
+TURN = 2.0 * math.pi
+
+
+def tile_list_corridor_advisory_scores_kernel(
+    tc, tab_words, tab_scales, offs, offs2, offs3, wa, wb, w4_words, w4_scales,
+    gain, w8_words, w8_scales, wind, wgo, out,
+):
+    nc = tc.nc
+    with ExitStack() as ctx:
+        keep = ctx.enter_context(tc.tile_pool(name="keep", bufs=1))
+        ring = ctx.enter_context(tc.tile_pool(name="ring", bufs=2))
+        psum = ctx.enter_context(tc.psum_pool(name="psum", bufs=2))
+
+        def kept(shape, dtype, name):
+            return keep.tile(shape, dtype, name=name, align_bytes=64)
+
+        tab_plane = kept([P, T], U8, "tab_plane")
+        nc.gpsimd.memset(tab_plane[:].bitcast(I32), 0)
+        w4_plane_raw = kept([P, PASSES, H], U8, "w4_plane_raw")
+        nc.vector.memset(w4_plane_raw[:].bitcast(I32), 0)
+        w8_plane = kept([P, N], U8, "w8_plane")
+        nc.vector.memset(w8_plane[:].bitcast(I32), 0)
+        low_plane = kept([P, S], U8, "low_plane")
+        nc.vector.memset(low_plane[:].bitcast(I32), 0)
+
+        lists = [kept([P, S // 16], U16, "list%d" % i) for i in range(3)]
+        nc.sync.dma_start(lists[0][:], offs)
+        nc.sync.dma_start(lists[1][:], offs2)
+        raw = {}
+
+        def load_weight(w, a):
+            raw[w, a] = ring.tile([P, PACK, H], F32, name="raw%d" % w, align_bytes=64, bufs=2 - w)
+            nc.sync.dma_start(raw[w, a][:], (wa, wb)[w][a * 512 : (a + 1) * 512, :].rearrange("(p j) c -> p j c", j=PACK))
+
+        load_weight(0, 0)
+        for q in range(4):
+            nc.sync.dma_start(
+                tab_plane[32 * q : 32 * q + 4 * PASSES, :].bitcast(I32),
+                tab_scales[:, 4 * q : 4 * q + 4, :].bitcast(I32))
+        load_weight(0, 1)
+        table = [kept([P, T], I32, "table%d" % a) for a in range(PASSES)]
+        for a in range(PASSES):
+            nc.sync.dma_start(table[a][:], tab_words[a].rearrange("p n t -> p (n t)").bitcast(I32))
+        load_weight(1, 0)
+        raw[1, 1] = [ring.tile([P, PACK, H // 2], F32, name="raw_half", align_bytes=64) for i in range(2)]
+        for i in range(2):
+            nc.sync.dma_start(raw[1, 1][i][:], wb[512:1024, i * 256 : (i + 1) * 256].rearrange("(p j) c -> p j c", j=PACK))
+        w4_raw = kept([P, PASSES, 2 * H], U8, "w4_raw")
+        nc.sync.dma_start(w4_raw[:].bitcast(I32), w4_words.rearrange("a p c -> p a c").bitcast(I32))
+        for q in range(4):
+            nc.sync.dma_start(
+                w4_plane_raw[32 * q : 32 * q + 4, :, :].bitcast(I32),
+                w4_scales[:, 4 * q : 4 * q + 4, :].rearrange("a r c -> r a c").bitcast(I32))
+        gains = kept([P, PACK], F32, "gains")
+        nc.sync.dma_start(gains[:], gain.rearrange("(p t) -> p t", t=PACK))
+        w8_codes = kept([P, N], I32, "w8_codes")
+        nc.sync.dma_start(w8_codes[:], w8_words[0].rearrange("p n t -> p (n t)").bitcast(I32))
+        for q in range(4):
+            nc.sync.dma_start(w8_plane[32 * q : 32 * q + 4, :].bitcast(I32), w8_scales[0, 4 * q : 4 * q + 4, :].bitcast(I32))
+        identity = kept([P, P], F32, "identity")
+        make_identity(nc, identity[:])
+
+        codes = {}
+        scales = {}
+
+        def quantise_weight(w, a):
+            rounded = ring.tile([P, PACK * H], BF16, name="rounded", align_bytes=64)
+            dst = rounded[:].rearrange("p (t m j) -> p m j t", t=PACK, j=PACK)
+            if (w, a) == (1, 1):
+                for i, copy in enumerate((nc.vector.tensor_copy, nc.scalar.copy)):
+                    copy(dst[:, 64 * i : 64 * (i + 1)], raw[w, a][i][:].rearrange("p j (m t) -> p m j t", t=PACK))
+            else:
+                copy = nc.scalar.copy if w == 0 else nc.vector.tensor_copy
+                copy(dst, raw[w, a][:].rearrange("p j (m t) -> p m j t", t=PACK))
+            codes[w, a] = kept([P, H], U32, "codes%d_%d" % (w, a))
+            scales[w, a] = kept([P, H], U8, "scales%d_%d" % (w, a))
+            nc.vector.quantize_mx(codes[w, a][:].bitcast(FP8X4), scales[w, a][:], rounded[:])
+
+        for a in range(PASSES):
+            quantise_weight(0, a)
+
+        planes = {}
+        words = {}
+        for li in range(2):
+            planes[li] = kept([P, S], U8, "plane%d" % li)
+            nc.vector.tensor_copy(planes[li][:], tab_plane[:].indirect(lists[li][:]))
+        for q in range(4):
+            nc.sync.dma_start(low_plane[32 * q : 32 * q + 4, :].bitcast(I32), planes[0][32 * q + 4 : 32 * q + 8, :].bitcast(I32))
+
+        winds = [ring.tile([P, BLOCKS, GROUP], F32, name="raw0", align_bytes=64) if g < 2 else kept([P, BLOCKS, GROUP], F32, "wind%d" % g) for g in range(GROUPS)]
+        factors = kept([P, S], F32, "factors")
+        wind_rows = wind.rearrange("(b p) s -> p b s", p=P)
+        nc.sync.dma_start(winds[0][:], wind_rows[:, :, 0:GROUP])
+        nc.sync.dma_start(lists[2][:], offs3)
+        nc.sync.dma_start(factors[:], wgo)
+        for g in range(1, GROUPS):
+            nc.sync.dma_start(winds[g][:], wind_rows[:, :, g * GROUP : (g + 1) * GROUP])
+
+        def gather_words(li, a, hf):
+            if (a, hf) == (1, 1):
+                words[li, a, hf] = ring.tile([P, HALF], U32, name="rounded", align_bytes=64)
+            else:
+                words[li, a, hf] = kept([P, HALF], U32, "words%d_%d_%d" % (li, a, hf))
+            nc.vector.tensor_copy(words[li, a, hf][:], table[a][:].bitcast(U32).indirect(lists[li][:, 32 * hf : 32 * hf + 32]))
+
+        for a, hf in ((0, 0), (0, 1), (1, 0)):
+            for li in range(2):
+                gather_words(li, a, hf)
+
+        for a in range(PASSES):
+            quantise_weight(1, a)
+        w4_codes = kept([P, PASSES, 2 * H], U8, "w4_codes")
+        nc.vector.tensor_copy(
+            w4_codes[:].bitcast(U16).rearrange("p a (t m) -> p a t m", t=PACK),
+            w4_raw[:].bitcast(U16).rearrange("p a (m t) -> p a t m", t=PACK))
+        w4_plane = kept([P, PASSES, H], U8, "w4_plane")
+        nc.vector.tensor_copy(
+            w4_plane[:].rearrange("p a (t m) -> p a t m", t=PACK),
+            w4_plane_raw[:].rearrange("p a (m t) -> p a t m", t=PACK))
+
+        for li in range(2):
+            gather_words(li, 1, 1)
+
+        pages = [kept([P, T2], F32, "page%d" % b if b < EARLY else "table%d" % (b - EARLY)) for b in range(BLOCKS)]
+        for b in range(BLOCKS):
+            nc.gpsimd.memset(pages[b][:], 0.0)
+
+        waves = {}
+        scores = kept([P, BLOCKS, S], F32, "scores")
+
+        def entries(g):
+            return g // 2, slice((g % 2) * GROUP, (g % 2 + 1) * GROUP)
+
+        def wave(w, g):
+            hf, cols = entries(g)
+            turns = ring.tile([P, 2, H], F32, name="turns")
+            for c in range(2):
+                first = cols.start + c * P
+                bank = psum.tile([P, H], F32, name="angle")
+                for a in range(PASSES):
+                    nc.tensor.matmul_mx(
+                        bank[:],
+                        lhsT=words[w, a, hf][:, first : first + P].bitcast(FP8X4),
+                        lhsT_scale=planes[w][4 * a : P, g * GROUP + c * P : g * GROUP + (c + 1) * P],
+                        rhs=codes[w, a][:].bitcast(FP8X4),
+                        rhs_scale=scales[w, a][:],
+                        start=(a == 0), stop=(a == PASSES - 1))
+                nc.scalar.activation(turns[:, c], bank[:], ACT.Copy, bias=0.25 * w, scale=1.0 / TURN)
+            shifted = ring.tile([P, 2, H], U32, name="shifted")
+            for c in range(2):
+                nc.scalar.activation(shifted[:, c], turns[:, c], ACT.Copy, bias=ROUNDER, scale=1.0)
+            wholes = ring.tile([P, 2, H], F32, name="wholes")
+            for c in range(2):
+                nc.scalar.activation(wholes[:, c], shifted[:, c], ACT.Copy, bias=ROUNDER, scale=-1.0)
+            waves[w, g] = ring.tile([P, PACK, GROUP], F32, name="wave%d" % w, bufs=3 - w)
+            for c in range(2):
+                bank = psum.tile([P, PACK, P], F32, name="rest")
+                for t in range(PACK):
+                    nc.tensor.matmul(bank[:, t, :], lhsT=turns[:, c, t * P : (t + 1) * P], rhs=identity[:], is_transpose=True, start=True, stop=False)
+                    nc.tensor.matmul(bank[:, t, :], lhsT=wholes[:, c, t * P : (t + 1) * P], rhs=identity[:], is_transpose=True, start=False, stop=True)
+                nc.scalar.activation(waves[w, g][:, :, c * P : (c + 1) * P], bank[:], ACT.Sin, scale=TURN)
+
+        quantised = {}
+
+        def middle(g):
+            hf, cols = entries(g)
+            for t in range(PACK):
+                nc.vector.scalar_tensor_tensor(waves[0, g][:, t], waves[0, g][:, t], gains[:, t : t + 1], waves[1, g][:, t], ALU.mult, ALU.mult)
+            h = ring.tile([P, GROUP * PACK], BF16, name="h", align_bytes=64)
+            for c in range(GROUP // P):
+                own = psum.tile([P, PACK, P], F32, name="own")
+                first = cols.start + c * P
+                for t in range(PACK):
+                    for a in range(PASSES):
+                        plane = planes[0] if a == 0 else low_plane
+                        nc.tensor.matmul_mx(
+                            own[:, t, :],
+                            lhsT=w4_codes[:, a, 2 * t * P : 2 * (t + 1) * P].bitcast(FP4X4),
+                            lhsT_scale=w4_plane[:, a, t * P : (t + 1) * P],
+                            rhs=words[0, a, hf][:, first : first + P].bitcast(FP8X4),
+                            rhs_scale=plane[:, g * GROUP + c * P : g * GROUP + (c + 1) * P],
+                            start=(a == 0), stop=(a == PASSES - 1))
+                nc.vector.tensor_tensor(
+                    h[:, c * P * PACK : (c + 1) * P * PACK].rearrange("p (n i t) -> p n t i", i=4, t=PACK),
+                    waves[0, g][:, :, c * P : (c + 1) * P].rearrange("p t (n i) -> p n t i", i=4),
+                    own[:].rearrange("p t (n i) -> p n t i", i=4),
+                    ALU.add)
+            h_codes = ring.tile([P, GROUP], U32, name="h_codes", align_bytes=64)
+            h_scales = ring.tile([P, GROUP], U8, name="h_scales", align_bytes=64)
+            nc.vector.quantize_mx(h_codes[:].bitcast(FP8X4), h_scales[:], h[:])
+            quantised[g] = (h_codes, h_scales)
+
+        def score(g, pair, tag):
+            h_codes, h_scales = quantised[g]
+            bank = psum.tile([P, 2, GROUP], F32, name=tag)
+            for i in range(2):
+                b = 2 * pair + i
+                nc.tensor.matmul_mx(
+                    bank[:, i, :],
+                    lhsT=w8_codes[:, b * P : (b + 1) * P].bitcast(FP8X4),
+                    lhsT_scale=w8_plane[:, b * P : (b + 1) * P],
+                    rhs=h_codes[:].bitcast(FP8X4), rhs_scale=h_scales[:],
+                    start=True, stop=True)
+            nc.vector.tensor_tensor(scores[:, 2 * pair : 2 * pair + 2, g * GROUP : (g + 1) * GROUP], bank[:], winds[g][:, 2 * pair : 2 * pair + 2, :], ALU.mult)
+
+        def place(b, first, count, values):
+            nc.vector.tensor_tensor(
+                pages[b][:].indirect(lists[2][:, first // 16 : (first + count) // 16]),
+                values, factors[:, first : first + count], ALU.mult)
+            if first + count == S:
+                nc.sync.dma_start(out[b * P : (b + 1) * P, :], pages[b][:])
+
+        for g in range(GROUPS):
+            cols = slice(g * GROUP, (g + 1) * GROUP)
+            wave(0, g)
+            wave(1, g)
+            middle(g)
+            if g > 0:
+                score(g - 1, 2, "own")
+            score(g, 0, "score")
+            score(g, 1, "score")
+            for part in (scores[:, 0, cols], scores[:, 1, cols], scores[:, 2:4, cols]):
+                nc.scalar.activation(part, part, ACT.Tanh)
+            if g == GROUPS - 1:
+                score(g, 2, "own")
+            for b in range(EARLY):
+                place(b, cols.start, GROUP, scores[:, b, cols])
+        for b in range(EARLY, BLOCKS):
+            nc.scalar.activation(scores[:, b], scores[:, b], ACT.Tanh)
+            place(b, 0, S, scores[:, b])

@@ -51,6 +51,9 @@ def tile_list_corridor_advisory_scores_kernel(
         nc.vector.memset(w8_plane[:].bitcast(I32), 0)
         low_plane = kept([P, S], U8, "low_plane")
         nc.vector.memset(low_plane[:].bitcast(I32), 0)
+        warm = kept([P, 1], F32, "warm")
+        nc.vector.memset(warm[:], 0.0)
+        nc.scalar.activation(warm[:], warm[:], ACT.Silu)
 
         lists = [kept([P, S // 16], U16, "list%d" % i) for i in range(3)]
         nc.sync.dma_start(lists[0][:], offs)
@@ -89,30 +92,33 @@ def tile_list_corridor_advisory_scores_kernel(
         identity = kept([P, P], F32, "identity")
         make_identity(nc, identity[:])
 
+        pages = [kept([P, T2], F32, "page%d" % b) for b in range(EARLY)]
+        for page in pages:
+            nc.vector.memset(page[:], 0.0)
+
         codes = {}
         scales = {}
 
         def quantise_weight(w, a):
             rounded = ring.tile([P, PACK * H], BF16, name="rounded", align_bytes=64)
-            dst = rounded[:].rearrange("p (t m j) -> p m j t", t=PACK, j=PACK)
+            dst = rounded[:].rearrange("p (c i j) -> p c j i", i=2, j=PACK)
             if (w, a) == (1, 1):
-                for i, copy in enumerate((nc.vector.tensor_copy, nc.scalar.copy)):
-                    copy(dst[:, 64 * i : 64 * (i + 1)], raw[w, a][i][:].rearrange("p j (m t) -> p m j t", t=PACK))
+                for i in range(2):
+                    nc.vector.tensor_copy(dst[:, P * i : P * (i + 1)], raw[w, a][i][:].rearrange("p j (c i) -> p c j i", i=2))
             else:
                 copy = nc.scalar.copy if w == 0 else nc.vector.tensor_copy
-                copy(dst, raw[w, a][:].rearrange("p j (m t) -> p m j t", t=PACK))
+                copy(dst, raw[w, a][:].rearrange("p j (c i) -> p c j i", i=2))
             codes[w, a] = kept([P, H], U32, "codes%d_%d" % (w, a))
             scales[w, a] = kept([P, H], U8, "scales%d_%d" % (w, a))
             nc.vector.quantize_mx(codes[w, a][:].bitcast(FP8X4), scales[w, a][:], rounded[:])
-
-        for a in range(PASSES):
-            quantise_weight(0, a)
 
         planes = {}
         words = {}
         for li in range(2):
             planes[li] = kept([P, S], U8, "plane%d" % li)
             nc.vector.tensor_copy(planes[li][:], tab_plane[:].indirect(lists[li][:]))
+        for a in range(PASSES):
+            quantise_weight(0, a)
         for q in range(4):
             nc.sync.dma_start(low_plane[32 * q : 32 * q + 4, :].bitcast(I32), planes[0][32 * q + 4 : 32 * q + 8, :].bitcast(I32))
 
@@ -126,15 +132,13 @@ def tile_list_corridor_advisory_scores_kernel(
             nc.sync.dma_start(winds[g][:], wind_rows[:, :, g * GROUP : (g + 1) * GROUP])
 
         def gather_words(li, a, hf):
-            if (a, hf) == (1, 1):
-                words[li, a, hf] = ring.tile([P, HALF], U32, name="rounded", align_bytes=64)
-            else:
-                words[li, a, hf] = kept([P, HALF], U32, "words%d_%d_%d" % (li, a, hf))
-            nc.vector.tensor_copy(words[li, a, hf][:], table[a][:].bitcast(U32).indirect(lists[li][:, 32 * hf : 32 * hf + 32]))
+            nc.vector.tensor_copy(words[li, hf][:, a, :], table[a][:].bitcast(U32).indirect(lists[li][:, 32 * hf : 32 * hf + 32]))
 
-        for a, hf in ((0, 0), (0, 1), (1, 0)):
+        for li in range(2):
+            words[li, 0] = kept([P, PASSES, HALF], U32, "words%d" % li)
+        for a in range(PASSES):
             for li in range(2):
-                gather_words(li, a, hf)
+                gather_words(li, a, 0)
 
         for a in range(PASSES):
             quantise_weight(1, a)
@@ -148,11 +152,14 @@ def tile_list_corridor_advisory_scores_kernel(
             w4_plane_raw[:].rearrange("p a (m t) -> p a t m", t=PACK))
 
         for li in range(2):
-            gather_words(li, 1, 1)
+            words[li, 1] = ring.tile([P, PASSES, HALF], U32, name="rounded", align_bytes=64)
+            for a in range(PASSES):
+                gather_words(li, a, 1)
 
-        pages = [kept([P, T2], F32, "page%d" % b if b < EARLY else "table%d" % (b - EARLY)) for b in range(BLOCKS)]
-        for b in range(BLOCKS):
-            nc.gpsimd.memset(pages[b][:], 0.0)
+        for b in range(EARLY, BLOCKS):
+            pages.append(kept([P, T2], F32, "table%d" % (b - EARLY)))
+            for first in range(0, T2, 512):
+                nc.gpsimd.memset(pages[b][:, first : first + 512], 0.0)
 
         waves = {}
         scores = kept([P, BLOCKS, S], F32, "scores")
@@ -169,12 +176,12 @@ def tile_list_corridor_advisory_scores_kernel(
                 for a in range(PASSES):
                     nc.tensor.matmul_mx(
                         bank[:],
-                        lhsT=words[w, a, hf][:, first : first + P].bitcast(FP8X4),
+                        lhsT=words[w, hf][:, a, first : first + P].bitcast(FP8X4),
                         lhsT_scale=planes[w][4 * a : P, g * GROUP + c * P : g * GROUP + (c + 1) * P],
                         rhs=codes[w, a][:].bitcast(FP8X4),
                         rhs_scale=scales[w, a][:],
                         start=(a == 0), stop=(a == PASSES - 1))
-                nc.scalar.activation(turns[:, c], bank[:], ACT.Copy, bias=0.25 * w, scale=1.0 / TURN)
+                nc.scalar.activation(turns[:, c].rearrange("p (t m) -> p t m", t=PACK), bank[:].rearrange("p (m t) -> p t m", t=PACK), ACT.Copy, bias=0.25 * w, scale=1.0 / TURN)
             shifted = ring.tile([P, 2, H], U32, name="shifted")
             for c in range(2):
                 nc.scalar.activation(shifted[:, c], turns[:, c], ACT.Copy, bias=ROUNDER, scale=1.0)
@@ -206,13 +213,13 @@ def tile_list_corridor_advisory_scores_kernel(
                             own[:, t, :],
                             lhsT=w4_codes[:, a, 2 * t * P : 2 * (t + 1) * P].bitcast(FP4X4),
                             lhsT_scale=w4_plane[:, a, t * P : (t + 1) * P],
-                            rhs=words[0, a, hf][:, first : first + P].bitcast(FP8X4),
+                            rhs=words[0, hf][:, a, first : first + P].bitcast(FP8X4),
                             rhs_scale=plane[:, g * GROUP + c * P : g * GROUP + (c + 1) * P],
                             start=(a == 0), stop=(a == PASSES - 1))
                 nc.vector.tensor_tensor(
-                    h[:, c * P * PACK : (c + 1) * P * PACK].rearrange("p (n i t) -> p n t i", i=4, t=PACK),
-                    waves[0, g][:, :, c * P : (c + 1) * P].rearrange("p t (n i) -> p n t i", i=4),
-                    own[:].rearrange("p t (n i) -> p n t i", i=4),
+                    h[:, c * P * PACK : (c + 1) * P * PACK].rearrange("p (n i t) -> p n t i", i=2, t=PACK),
+                    waves[0, g][:, :, c * P : (c + 1) * P].rearrange("p t (n i) -> p n t i", i=2),
+                    own[:].rearrange("p t (n i) -> p n t i", i=2),
                     ALU.add)
             h_codes = ring.tile([P, GROUP], U32, name="h_codes", align_bytes=64)
             h_scales = ring.tile([P, GROUP], U8, name="h_scales", align_bytes=64)

@@ -2,7 +2,6 @@ import math
 from contextlib import ExitStack
 
 import concourse.mybir as mybir
-from concourse.masks import make_identity
 
 K, T, S, H, N, T2 = 1024, 4096, 1024, 512, 768, 2048
 FLOPS = 2 * (3 * K * H * S + H * N * S)
@@ -20,12 +19,16 @@ ACT = mybir.ActivationFunctionType
 
 P = 128
 PACK = 4
-PASSES = K // (P * PACK)
-HALF = 512
+K_PASS = P * PACK
+PASSES = K // K_PASS
+QUADRANTS = 4
+PER_COLUMN = 16
+HALF = S // 2
 GROUP = 256
 GROUPS = S // GROUP
 BLOCKS = N // P
 EARLY = 4
+CLEAR = 512
 ROUNDER = 1.5 * 2**23
 TURN = 2.0 * math.pi
 
@@ -43,43 +46,51 @@ def tile_list_corridor_advisory_scores_kernel(
         def kept(shape, dtype, name):
             return keep.tile(shape, dtype, name=name, align_bytes=64)
 
+        def list_columns(first, count):
+            return slice(first // PER_COLUMN, (first + count) // PER_COLUMN)
+
         tab_plane = kept([P, T], U8, "tab_plane")
         nc.gpsimd.memset(tab_plane[:].bitcast(I32), 0)
         w4_plane_raw = kept([P, PASSES, H], U8, "w4_plane_raw")
         nc.vector.memset(w4_plane_raw[:].bitcast(I32), 0)
         w8_plane = kept([P, N], U8, "w8_plane")
         nc.vector.memset(w8_plane[:].bitcast(I32), 0)
-        low_plane = kept([P, S], U8, "low_plane")
-        nc.vector.memset(low_plane[:].bitcast(I32), 0)
+        second_pass_plane = kept([P, S], U8, "second_pass_plane")
+        nc.vector.memset(second_pass_plane[:].bitcast(I32), 0)
+
         warm = kept([P, 1], F32, "warm")
         nc.vector.memset(warm[:], 0.0)
         nc.scalar.activation(warm[:], warm[:], ACT.Silu)
 
-        lists = [kept([P, S // 16], U16, "list%d" % i) for i in range(3)]
+        lists = [kept([P, S // PER_COLUMN], U16, "list%d" % i) for i in range(3)]
         nc.sync.dma_start(lists[0][:], offs)
         nc.sync.dma_start(lists[1][:], offs2)
+        table = [kept([P, T], I32, "table%d" % a) for a in range(PASSES)]
         raw = {}
 
-        def load_weight(w, a):
-            raw[w, a] = ring.tile([P, PACK, H], F32, name="raw%d" % w, align_bytes=64, bufs=2 - w)
-            nc.sync.dma_start(raw[w, a][:], (wa, wb)[w][a * 512 : (a + 1) * 512, :].rearrange("(p j) c -> p j c", j=PACK))
+        def load_weight(side, a, first, width, tag):
+            piece = ring.tile([P, PACK, width], F32, name=tag, align_bytes=64, bufs=1 if tag == "raw_wb" else 2)
+            rows = (wa, wb)[side][a * K_PASS : (a + 1) * K_PASS, first : first + width]
+            nc.sync.dma_start(piece[:], rows.rearrange("(p j) c -> p j c", j=PACK))
+            raw.setdefault((side, a), []).append(piece)
 
-        load_weight(0, 0)
-        for q in range(4):
+        def load_table(a):
+            nc.sync.dma_start(table[a][:], tab_words[a].rearrange("p n t -> p (n t)").bitcast(I32))
+
+        load_weight(0, 0, 0, H, "raw_wa")
+        for q in range(QUADRANTS):
             nc.sync.dma_start(
                 tab_plane[32 * q : 32 * q + 4 * PASSES, :].bitcast(I32),
                 tab_scales[:, 4 * q : 4 * q + 4, :].bitcast(I32))
-        load_weight(0, 1)
-        table = [kept([P, T], I32, "table%d" % a) for a in range(PASSES)]
-        for a in range(PASSES):
-            nc.sync.dma_start(table[a][:], tab_words[a].rearrange("p n t -> p (n t)").bitcast(I32))
-        load_weight(1, 0)
-        raw[1, 1] = [ring.tile([P, PACK, H // 2], F32, name="raw_half", align_bytes=64) for i in range(2)]
-        for i in range(2):
-            nc.sync.dma_start(raw[1, 1][i][:], wb[512:1024, i * 256 : (i + 1) * 256].rearrange("(p j) c -> p j c", j=PACK))
+        load_table(0)
+        load_weight(0, 1, 0, H, "raw_wa")
+        load_weight(1, 0, 0, H, "raw_wb")
+        load_table(1)
+        load_weight(1, 1, 0, H // 2, "raw_half")
+        load_weight(1, 1, H // 2, H // 2, "raw_half")
         w4_raw = kept([P, PASSES, 2 * H], U8, "w4_raw")
         nc.sync.dma_start(w4_raw[:].bitcast(I32), w4_words.rearrange("a p c -> p a c").bitcast(I32))
-        for q in range(4):
+        for q in range(QUADRANTS):
             nc.sync.dma_start(
                 w4_plane_raw[32 * q : 32 * q + 4, :, :].bitcast(I32),
                 w4_scales[:, 4 * q : 4 * q + 4, :].rearrange("a r c -> r a c").bitcast(I32))
@@ -87,10 +98,9 @@ def tile_list_corridor_advisory_scores_kernel(
         nc.sync.dma_start(gains[:], gain.rearrange("(p t) -> p t", t=PACK))
         w8_codes = kept([P, N], I32, "w8_codes")
         nc.sync.dma_start(w8_codes[:], w8_words[0].rearrange("p n t -> p (n t)").bitcast(I32))
-        for q in range(4):
-            nc.sync.dma_start(w8_plane[32 * q : 32 * q + 4, :].bitcast(I32), w8_scales[0, 4 * q : 4 * q + 4, :].bitcast(I32))
-        identity = kept([P, P], F32, "identity")
-        make_identity(nc, identity[:])
+        for q in range(QUADRANTS):
+            nc.sync.dma_start(
+                w8_plane[32 * q : 32 * q + 4, :].bitcast(I32), w8_scales[0, 4 * q : 4 * q + 4, :].bitcast(I32))
 
         pages = [kept([P, T2], F32, "page%d" % b) for b in range(EARLY)]
         for page in pages:
@@ -99,30 +109,31 @@ def tile_list_corridor_advisory_scores_kernel(
         codes = {}
         scales = {}
 
-        def quantise_weight(w, a):
+        def quantise_weight(side, a):
             rounded = ring.tile([P, PACK * H], BF16, name="rounded", align_bytes=64)
-            dst = rounded[:].rearrange("p (c i j) -> p c j i", i=2, j=PACK)
-            if (w, a) == (1, 1):
-                for i in range(2):
-                    nc.vector.tensor_copy(dst[:, P * i : P * (i + 1)], raw[w, a][i][:].rearrange("p j (c i) -> p c j i", i=2))
-            else:
-                copy = nc.scalar.copy if w == 0 else nc.vector.tensor_copy
-                copy(dst, raw[w, a][:].rearrange("p j (c i) -> p c j i", i=2))
-            codes[w, a] = kept([P, H], U32, "codes%d_%d" % (w, a))
-            scales[w, a] = kept([P, H], U8, "scales%d_%d" % (w, a))
-            nc.vector.quantize_mx(codes[w, a][:].bitcast(FP8X4), scales[w, a][:], rounded[:])
+            dealt = rounded[:].rearrange("p (t m j) -> p m t j", t=PACK, j=PACK)
+            share = P // len(raw[side, a])
+            for i, piece in enumerate(raw[side, a]):
+                nc.scalar.copy(
+                    dealt[:, share * i : share * (i + 1)], piece[:].rearrange("p j (m t) -> p m t j", t=PACK))
+            codes[side, a] = kept([P, H], U32, "codes%d_%d" % (side, a))
+            scales[side, a] = kept([P, H], U8, "scales%d_%d" % (side, a))
+            nc.vector.quantize_mx(codes[side, a][:].bitcast(FP8X4), scales[side, a][:], rounded[:])
 
-        planes = {}
-        words = {}
-        for li in range(2):
-            planes[li] = kept([P, S], U8, "plane%d" % li)
-            nc.vector.tensor_copy(planes[li][:], tab_plane[:].indirect(lists[li][:]))
+        planes = [kept([P, S], U8, "plane%d" % side) for side in range(2)]
+        for side in range(2):
+            nc.vector.tensor_copy(planes[side][:], tab_plane[:].indirect(lists[side][:]))
         for a in range(PASSES):
             quantise_weight(0, a)
-        for q in range(4):
-            nc.sync.dma_start(low_plane[32 * q : 32 * q + 4, :].bitcast(I32), planes[0][32 * q + 4 : 32 * q + 8, :].bitcast(I32))
+        for q in range(QUADRANTS):
+            nc.sync.dma_start(
+                second_pass_plane[32 * q : 32 * q + 4, :].bitcast(I32),
+                planes[0][32 * q + 4 : 32 * q + 8, :].bitcast(I32))
 
-        winds = [ring.tile([P, BLOCKS, GROUP], F32, name="raw0", align_bytes=64) if g < 2 else kept([P, BLOCKS, GROUP], F32, "wind%d" % g) for g in range(GROUPS)]
+        winds = [
+            ring.tile([P, BLOCKS, GROUP], F32, name="raw_wa", align_bytes=64) if g < PASSES
+            else kept([P, BLOCKS, GROUP], F32, "wind%d" % g)
+            for g in range(GROUPS)]
         factors = kept([P, S], F32, "factors")
         wind_rows = wind.rearrange("(b p) s -> p b s", p=P)
         nc.sync.dma_start(winds[0][:], wind_rows[:, :, 0:GROUP])
@@ -131,17 +142,21 @@ def tile_list_corridor_advisory_scores_kernel(
         for g in range(1, GROUPS):
             nc.sync.dma_start(winds[g][:], wind_rows[:, :, g * GROUP : (g + 1) * GROUP])
 
-        def gather_words(li, a, hf):
-            nc.vector.tensor_copy(words[li, hf][:, a, :], table[a][:].bitcast(U32).indirect(lists[li][:, 32 * hf : 32 * hf + 32]))
+        words = {}
 
-        for li in range(2):
-            words[li, 0] = kept([P, PASSES, HALF], U32, "words%d" % li)
+        def gather_words(side, a, half):
+            nc.vector.tensor_copy(
+                words[side, half][:, a, :],
+                table[a][:].bitcast(U32).indirect(lists[side][:, list_columns(half * HALF, HALF)]))
+
+        for side in range(2):
+            words[side, 0] = kept([P, PASSES, HALF], U32, "words%d" % side)
         for a in range(PASSES):
-            for li in range(2):
-                gather_words(li, a, 0)
-
+            for side in range(2):
+                gather_words(side, a, 0)
         for a in range(PASSES):
             quantise_weight(1, a)
+
         w4_codes = kept([P, PASSES, 2 * H], U8, "w4_codes")
         nc.vector.tensor_copy(
             w4_codes[:].bitcast(U16).rearrange("p a (t m) -> p a t m", t=PACK),
@@ -151,116 +166,113 @@ def tile_list_corridor_advisory_scores_kernel(
             w4_plane[:].rearrange("p a (t m) -> p a t m", t=PACK),
             w4_plane_raw[:].rearrange("p a (m t) -> p a t m", t=PACK))
 
-        for li in range(2):
-            words[li, 1] = ring.tile([P, PASSES, HALF], U32, name="rounded", align_bytes=64)
+        for side in range(2):
+            words[side, 1] = ring.tile([P, PASSES, HALF], U32, name="rounded", align_bytes=64)
             for a in range(PASSES):
-                gather_words(li, a, 1)
+                gather_words(side, a, 1)
 
         for b in range(EARLY, BLOCKS):
             pages.append(kept([P, T2], F32, "table%d" % (b - EARLY)))
-            for first in range(0, T2, 512):
-                nc.gpsimd.memset(pages[b][:, first : first + 512], 0.0)
+            for first in range(0, T2, CLEAR):
+                nc.gpsimd.memset(pages[b][:, first : first + CLEAR], 0.0)
 
         waves = {}
+        quantised_h = {}
         scores = kept([P, BLOCKS, S], F32, "scores")
 
-        def entries(g):
-            return g // 2, slice((g % 2) * GROUP, (g % 2 + 1) * GROUP)
+        def group_words(side, a, g, first, count):
+            start = g * GROUP % HALF + first
+            return words[side, g * GROUP // HALF][:, a, start : start + count].bitcast(FP8X4)
 
-        def wave(w, g):
-            hf, cols = entries(g)
-            turns = ring.tile([P, 2, H], F32, name="turns")
-            for c in range(2):
-                first = cols.start + c * P
-                bank = psum.tile([P, H], F32, name="angle")
-                for a in range(PASSES):
-                    nc.tensor.matmul_mx(
-                        bank[:],
-                        lhsT=words[w, hf][:, a, first : first + P].bitcast(FP8X4),
-                        lhsT_scale=planes[w][4 * a : P, g * GROUP + c * P : g * GROUP + (c + 1) * P],
-                        rhs=codes[w, a][:].bitcast(FP8X4),
-                        rhs_scale=scales[w, a][:],
-                        start=(a == 0), stop=(a == PASSES - 1))
-                nc.scalar.activation(turns[:, c].rearrange("p (t m) -> p t m", t=PACK), bank[:].rearrange("p (m t) -> p t m", t=PACK), ACT.Copy, bias=0.25 * w, scale=1.0 / TURN)
-            shifted = ring.tile([P, 2, H], U32, name="shifted")
-            for c in range(2):
-                nc.scalar.activation(shifted[:, c], turns[:, c], ACT.Copy, bias=ROUNDER, scale=1.0)
-            wholes = ring.tile([P, 2, H], F32, name="wholes")
-            for c in range(2):
-                nc.scalar.activation(wholes[:, c], shifted[:, c], ACT.Copy, bias=ROUNDER, scale=-1.0)
-            waves[w, g] = ring.tile([P, PACK, GROUP], F32, name="wave%d" % w, bufs=3 - w)
-            for c in range(2):
-                bank = psum.tile([P, PACK, P], F32, name="rest")
-                for t in range(PACK):
-                    nc.tensor.matmul(bank[:, t, :], lhsT=turns[:, c, t * P : (t + 1) * P], rhs=identity[:], is_transpose=True, start=True, stop=False)
-                    nc.tensor.matmul(bank[:, t, :], lhsT=wholes[:, c, t * P : (t + 1) * P], rhs=identity[:], is_transpose=True, start=False, stop=True)
-                nc.scalar.activation(waves[w, g][:, :, c * P : (c + 1) * P], bank[:], ACT.Sin, scale=TURN)
+        def wave(side, g):
+            entries = slice(g * GROUP, (g + 1) * GROUP)
+            waves[side, g] = ring.tile([P, PACK, GROUP], F32, name="wave%d" % side, bufs=3 - side)
+            shifted = ring.tile([P, PACK, GROUP], U32, name="shifted")
+            pairs = (slice(0, 2), slice(2, 4))
+            for pair in pairs:
+                bank = psum.tile([P, 2, GROUP], F32, name="angle", bufs=4)
+                for i in range(2):
+                    run = slice((pair.start + i) * P, (pair.start + i + 1) * P)
+                    for a in range(PASSES):
+                        nc.tensor.matmul_mx(
+                            bank[:, i, :],
+                            lhsT=codes[side, a][:, run].bitcast(FP8X4), lhsT_scale=scales[side, a][:, run],
+                            rhs=group_words(side, a, g, 0, GROUP), rhs_scale=planes[side][4 * a : P, entries],
+                            start=(a == 0), stop=(a == PASSES - 1))
+                nc.scalar.activation(waves[side, g][:, pair], bank[:], ACT.Copy, bias=0.25 * side, scale=1.0 / TURN)
+            for pair in pairs:
+                nc.scalar.activation(shifted[:, pair], waves[side, g][:, pair], ACT.Copy, bias=ROUNDER, scale=1.0)
+            for pair in pairs:
+                nc.vector.scalar_tensor_tensor(
+                    waves[side, g][:, pair], shifted[:, pair].bitcast(I32), ROUNDER, waves[side, g][:, pair],
+                    ALU.subtract, ALU.subtract)
+            for pair in pairs:
+                nc.scalar.activation(waves[side, g][:, pair], waves[side, g][:, pair], ACT.Sin, scale=-TURN)
 
-        quantised = {}
-
-        def middle(g):
-            hf, cols = entries(g)
+        def make_h(g):
+            product = waves[0, g]
             for t in range(PACK):
-                nc.vector.scalar_tensor_tensor(waves[0, g][:, t], waves[0, g][:, t], gains[:, t : t + 1], waves[1, g][:, t], ALU.mult, ALU.mult)
+                nc.vector.scalar_tensor_tensor(
+                    product[:, t], waves[0, g][:, t], gains[:, t : t + 1], waves[1, g][:, t], ALU.mult, ALU.mult)
             h = ring.tile([P, GROUP * PACK], BF16, name="h", align_bytes=64)
-            for c in range(GROUP // P):
+            for first in range(0, GROUP, P):
                 own = psum.tile([P, PACK, P], F32, name="own")
-                first = cols.start + c * P
+                entries = slice(g * GROUP + first, g * GROUP + first + P)
                 for t in range(PACK):
                     for a in range(PASSES):
-                        plane = planes[0] if a == 0 else low_plane
                         nc.tensor.matmul_mx(
                             own[:, t, :],
                             lhsT=w4_codes[:, a, 2 * t * P : 2 * (t + 1) * P].bitcast(FP4X4),
                             lhsT_scale=w4_plane[:, a, t * P : (t + 1) * P],
-                            rhs=words[0, hf][:, a, first : first + P].bitcast(FP8X4),
-                            rhs_scale=plane[:, g * GROUP + c * P : g * GROUP + (c + 1) * P],
+                            rhs=group_words(0, a, g, first, P),
+                            rhs_scale=(planes[0], second_pass_plane)[a][:, entries],
                             start=(a == 0), stop=(a == PASSES - 1))
                 nc.vector.tensor_tensor(
-                    h[:, c * P * PACK : (c + 1) * P * PACK].rearrange("p (n i t) -> p n t i", i=2, t=PACK),
-                    waves[0, g][:, :, c * P : (c + 1) * P].rearrange("p t (n i) -> p n t i", i=2),
+                    h[:, first * PACK : (first + P) * PACK].rearrange("p (n i t) -> p n t i", i=2, t=PACK),
+                    product[:, :, first : first + P].rearrange("p t (n i) -> p n t i", i=2),
                     own[:].rearrange("p t (n i) -> p n t i", i=2),
                     ALU.add)
             h_codes = ring.tile([P, GROUP], U32, name="h_codes", align_bytes=64)
             h_scales = ring.tile([P, GROUP], U8, name="h_scales", align_bytes=64)
             nc.vector.quantize_mx(h_codes[:].bitcast(FP8X4), h_scales[:], h[:])
-            quantised[g] = (h_codes, h_scales)
+            quantised_h[g] = (h_codes, h_scales)
 
-        def score(g, pair, tag):
-            h_codes, h_scales = quantised[g]
+        def score(g, first_block, tag):
+            h_codes, h_scales = quantised_h[g]
+            blocks = slice(first_block, first_block + 2)
             bank = psum.tile([P, 2, GROUP], F32, name=tag)
             for i in range(2):
-                b = 2 * pair + i
+                rows = slice((first_block + i) * P, (first_block + i + 1) * P)
                 nc.tensor.matmul_mx(
                     bank[:, i, :],
-                    lhsT=w8_codes[:, b * P : (b + 1) * P].bitcast(FP8X4),
-                    lhsT_scale=w8_plane[:, b * P : (b + 1) * P],
+                    lhsT=w8_codes[:, rows].bitcast(FP8X4), lhsT_scale=w8_plane[:, rows],
                     rhs=h_codes[:].bitcast(FP8X4), rhs_scale=h_scales[:],
                     start=True, stop=True)
-            nc.vector.tensor_tensor(scores[:, 2 * pair : 2 * pair + 2, g * GROUP : (g + 1) * GROUP], bank[:], winds[g][:, 2 * pair : 2 * pair + 2, :], ALU.mult)
-
-        def place(b, first, count, values):
             nc.vector.tensor_tensor(
-                pages[b][:].indirect(lists[2][:, first // 16 : (first + count) // 16]),
-                values, factors[:, first : first + count], ALU.mult)
+                scores[:, blocks, g * GROUP : (g + 1) * GROUP], bank[:], winds[g][:, blocks, :], ALU.mult)
+
+        def place(b, first, count):
+            nc.vector.tensor_tensor(
+                pages[b][:].indirect(lists[2][:, list_columns(first, count)]),
+                scores[:, b, first : first + count], factors[:, first : first + count], ALU.mult)
             if first + count == S:
                 nc.sync.dma_start(out[b * P : (b + 1) * P, :], pages[b][:])
 
         for g in range(GROUPS):
-            cols = slice(g * GROUP, (g + 1) * GROUP)
+            entries = slice(g * GROUP, (g + 1) * GROUP)
             wave(0, g)
             wave(1, g)
-            middle(g)
+            make_h(g)
             if g > 0:
-                score(g - 1, 2, "own")
-            score(g, 0, "score")
-            score(g, 1, "score")
-            for part in (scores[:, 0, cols], scores[:, 1, cols], scores[:, 2:4, cols]):
+                score(g - 1, EARLY, "own")
+            for b in range(0, EARLY, 2):
+                score(g, b, "score")
+            for part in (scores[:, 0, entries], scores[:, 1, entries], scores[:, 2:EARLY, entries]):
                 nc.scalar.activation(part, part, ACT.Tanh)
             if g == GROUPS - 1:
-                score(g, 2, "own")
+                score(g, EARLY, "own")
             for b in range(EARLY):
-                place(b, cols.start, GROUP, scores[:, b, cols])
+                place(b, entries.start, GROUP)
         for b in range(EARLY, BLOCKS):
             nc.scalar.activation(scores[:, b], scores[:, b], ACT.Tanh)
-            place(b, 0, S, scores[:, b])
+            place(b, 0, S)

@@ -27,7 +27,8 @@ HALF = S // 2
 GROUP = 256
 GROUPS = S // GROUP
 BLOCKS = N // P
-EARLY = 4
+EARLY = 2
+PAGES = 3
 CLEAR = 512
 ROUNDER = 1.5 * 2**23
 TURN = 2.0 * math.pi
@@ -77,19 +78,19 @@ def tile_list_corridor_advisory_scores_kernel(
         def load_table(a):
             nc.sync.dma_start(table[a][:], tab_words[a].rearrange("p n t -> p (n t)").bitcast(I32))
 
-        load_weight(0, 0, 0, H, "raw_wa")
+        w4_raw = kept([P, PASSES, 2 * H], U8, "w4_raw")
+        nc.sync.dma_start(w4_raw[:].bitcast(I32), w4_words.rearrange("a p c -> p a c").bitcast(I32))
         for q in range(QUADRANTS):
             nc.sync.dma_start(
                 tab_plane[32 * q : 32 * q + 4 * PASSES, :].bitcast(I32),
                 tab_scales[:, 4 * q : 4 * q + 4, :].bitcast(I32))
+        load_weight(0, 0, 0, H, "raw_wa")
         load_table(0)
+        load_table(1)
         load_weight(0, 1, 0, H, "raw_wa")
         load_weight(1, 0, 0, H, "raw_wb")
-        load_table(1)
         load_weight(1, 1, 0, H // 2, "raw_half")
         load_weight(1, 1, H // 2, H // 2, "raw_half")
-        w4_raw = kept([P, PASSES, 2 * H], U8, "w4_raw")
-        nc.sync.dma_start(w4_raw[:].bitcast(I32), w4_words.rearrange("a p c -> p a c").bitcast(I32))
         for q in range(QUADRANTS):
             nc.sync.dma_start(
                 w4_plane_raw[32 * q : 32 * q + 4, :, :].bitcast(I32),
@@ -102,9 +103,9 @@ def tile_list_corridor_advisory_scores_kernel(
             nc.sync.dma_start(
                 w8_plane[32 * q : 32 * q + 4, :].bitcast(I32), w8_scales[0, 4 * q : 4 * q + 4, :].bitcast(I32))
 
-        pages = [kept([P, T2], F32, "page%d" % b) for b in range(EARLY)]
+        pages = [kept([P, T2], F32, "page%d" % b) for b in range(PAGES)]
         for page in pages:
-            nc.vector.memset(page[:], 0.0)
+            nc.gpsimd.memset(page[:], 0.0)
 
         codes = {}
         scales = {}
@@ -114,7 +115,7 @@ def tile_list_corridor_advisory_scores_kernel(
             dealt = rounded[:].rearrange("p (t m j) -> p m t j", t=PACK, j=PACK)
             share = P // len(raw[side, a])
             for i, piece in enumerate(raw[side, a]):
-                nc.scalar.copy(
+                (nc.vector.tensor_copy if (side, a, i) in ((1, 1, 1),) else nc.scalar.copy)(
                     dealt[:, share * i : share * (i + 1)], piece[:].rearrange("p j (m t) -> p m t j", t=PACK))
             codes[side, a] = kept([P, H], U32, "codes%d_%d" % (side, a))
             scales[side, a] = kept([P, H], U8, "scales%d_%d" % (side, a))
@@ -143,17 +144,10 @@ def tile_list_corridor_advisory_scores_kernel(
             nc.sync.dma_start(winds[g][:], wind_rows[:, :, g * GROUP : (g + 1) * GROUP])
 
         words = {}
-
-        def gather_words(side, a, half):
-            nc.vector.tensor_copy(
-                words[side, half][:, a, :],
-                table[a][:].bitcast(U32).indirect(lists[side][:, list_columns(half * HALF, HALF)]))
-
-        for side in range(2):
-            words[side, 0] = kept([P, PASSES, HALF], U32, "words%d" % side)
         for a in range(PASSES):
             for side in range(2):
-                gather_words(side, a, 0)
+                words[side, a] = kept([P, S], U32, "words%d_%d" % (side, a))
+                nc.vector.tensor_copy(words[side, a][:], table[a][:].bitcast(U32).indirect(lists[side][:]))
         for a in range(PASSES):
             quantise_weight(1, a)
 
@@ -166,23 +160,12 @@ def tile_list_corridor_advisory_scores_kernel(
             w4_plane[:].rearrange("p a (t m) -> p a t m", t=PACK),
             w4_plane_raw[:].rearrange("p a (m t) -> p a t m", t=PACK))
 
-        for side in range(2):
-            words[side, 1] = ring.tile([P, PASSES, HALF], U32, name="rounded", align_bytes=64)
-            for a in range(PASSES):
-                gather_words(side, a, 1)
-
-        for b in range(EARLY, BLOCKS):
-            pages.append(kept([P, T2], F32, "table%d" % (b - EARLY)))
-            for first in range(0, T2, CLEAR):
-                nc.gpsimd.memset(pages[b][:, first : first + CLEAR], 0.0)
-
         waves = {}
         quantised_h = {}
         scores = kept([P, BLOCKS, S], F32, "scores")
 
         def group_words(side, a, g, first, count):
-            start = g * GROUP % HALF + first
-            return words[side, g * GROUP // HALF][:, a, start : start + count].bitcast(FP8X4)
+            return words[side, a][:, g * GROUP + first : g * GROUP + first + count].bitcast(FP8X4)
 
         def wave(side, g):
             entries = slice(g * GROUP, (g + 1) * GROUP)
@@ -190,7 +173,7 @@ def tile_list_corridor_advisory_scores_kernel(
             shifted = ring.tile([P, PACK, GROUP], U32, name="shifted")
             pairs = (slice(0, 2), slice(2, 4))
             for pair in pairs:
-                bank = psum.tile([P, 2, GROUP], F32, name="angle", bufs=4)
+                bank = psum.tile([P, 2, GROUP], F32, name="angle", bufs=3)
                 for i in range(2):
                     run = slice((pair.start + i) * P, (pair.start + i + 1) * P)
                     for a in range(PASSES):
@@ -201,7 +184,10 @@ def tile_list_corridor_advisory_scores_kernel(
                             start=(a == 0), stop=(a == PASSES - 1))
                 nc.scalar.activation(waves[side, g][:, pair], bank[:], ACT.Copy, bias=0.25 * side, scale=1.0 / TURN)
             for pair in pairs:
-                nc.scalar.activation(shifted[:, pair], waves[side, g][:, pair], ACT.Copy, bias=ROUNDER, scale=1.0)
+                if (side, g) in ((0, 0), (1, 0)):
+                    nc.vector.tensor_scalar(shifted[:, pair].bitcast(I32), waves[side, g][:, pair], ROUNDER, None, ALU.add)
+                else:
+                    nc.scalar.activation(shifted[:, pair], waves[side, g][:, pair], ACT.Copy, bias=ROUNDER, scale=1.0)
             for pair in pairs:
                 nc.vector.scalar_tensor_tensor(
                     waves[side, g][:, pair], shifted[:, pair].bitcast(I32), ROUNDER, waves[side, g][:, pair],
@@ -240,7 +226,7 @@ def tile_list_corridor_advisory_scores_kernel(
         def score(g, first_block, tag):
             h_codes, h_scales = quantised_h[g]
             blocks = slice(first_block, first_block + 2)
-            bank = psum.tile([P, 2, GROUP], F32, name=tag)
+            bank = psum.tile([P, 2, GROUP], F32, name=tag, bufs=3)
             for i in range(2):
                 rows = slice((first_block + i) * P, (first_block + i + 1) * P)
                 nc.tensor.matmul_mx(
@@ -253,26 +239,23 @@ def tile_list_corridor_advisory_scores_kernel(
 
         def place(b, first, count):
             nc.vector.tensor_tensor(
-                pages[b][:].indirect(lists[2][:, list_columns(first, count)]),
+                pages[b % PAGES][:].indirect(lists[2][:, list_columns(first, count)]),
                 scores[:, b, first : first + count], factors[:, first : first + count], ALU.mult)
             if first + count == S:
-                nc.sync.dma_start(out[b * P : (b + 1) * P, :], pages[b][:])
+                nc.sync.dma_start(out[b * P : (b + 1) * P, :], pages[b % PAGES][:])
+
+        def bound_and_place(b, first, count):
+            part = scores[:, b, first : first + count]
+            nc.scalar.activation(part, part, ACT.Tanh)
+            place(b, first, count)
 
         for g in range(GROUPS):
-            entries = slice(g * GROUP, (g + 1) * GROUP)
             wave(0, g)
             wave(1, g)
             make_h(g)
-            if g > 0:
-                score(g - 1, EARLY, "own")
-            for b in range(0, EARLY, 2):
+            for b in range(0, BLOCKS, 2):
                 score(g, b, "score")
-            for part in (scores[:, 0, entries], scores[:, 1, entries], scores[:, 2:EARLY, entries]):
-                nc.scalar.activation(part, part, ACT.Tanh)
-            if g == GROUPS - 1:
-                score(g, EARLY, "own")
-            for b in range(EARLY):
-                place(b, entries.start, GROUP)
+            for b, first, count in {1: [(0, 0, 512), (1, 0, 512)], 3: [(0, 512, 512), (1, 512, 512)]}.get(g, ()):
+                bound_and_place(b, first, count)
         for b in range(EARLY, BLOCKS):
-            nc.scalar.activation(scores[:, b], scores[:, b], ACT.Tanh)
-            place(b, 0, S)
+            bound_and_place(b, 0, S)

import math
from contextlib import ExitStack

import concourse.mybir as mybir

K, T, S, H, N, T2 = 1024, 4096, 1024, 512, 768, 2048
FLOPS = 2 * (3 * K * H * S + H * N * S)

F32 = mybir.dt.float32
BF16 = mybir.dt.bfloat16
I32 = mybir.dt.int32
U32 = mybir.dt.uint32
U16 = mybir.dt.uint16
U8 = mybir.dt.uint8
FP8X4 = mybir.dt.float8_e4m3fn_x4
FP4X4 = mybir.dt.float4_e2m1fn_x4
ALU = mybir.AluOpType
ACT = mybir.ActivationFunctionType

P = 128
PACK = 4
K_PASS = P * PACK
PASSES = K // K_PASS
QUADRANTS = 4
PER_COLUMN = 16
HALF = S // 2
GROUP = 256
GROUPS = S // GROUP
BLOCKS = N // P
EARLY = 2
PAGES = 3
CLEAR = 512
ROUNDER = 1.5 * 2**23
TURN = 2.0 * math.pi


def tile_list_corridor_advisory_scores_kernel(
    tc, tab_words, tab_scales, offs, offs2, offs3, wa, wb, w4_words, w4_scales,
    gain, w8_words, w8_scales, wind, wgo, out,
):
    nc = tc.nc
    with ExitStack() as ctx:
        keep = ctx.enter_context(tc.tile_pool(name="keep", bufs=1))
        ring = ctx.enter_context(tc.tile_pool(name="ring", bufs=2))
        psum = ctx.enter_context(tc.psum_pool(name="psum", bufs=2))

        def kept(shape, dtype, name):
            return keep.tile(shape, dtype, name=name, align_bytes=64)

        def list_columns(first, count):
            return slice(first // PER_COLUMN, (first + count) // PER_COLUMN)

        tab_plane = kept([P, T], U8, "tab_plane")
        nc.gpsimd.memset(tab_plane[:].bitcast(I32), 0)
        w4_plane_raw = kept([P, PASSES, H], U8, "w4_plane_raw")
        nc.vector.memset(w4_plane_raw[:].bitcast(I32), 0)
        w8_plane = kept([P, N], U8, "w8_plane")
        nc.vector.memset(w8_plane[:].bitcast(I32), 0)
        second_pass_plane = kept([P, S], U8, "second_pass_plane")
        nc.vector.memset(second_pass_plane[:].bitcast(I32), 0)

        warm = kept([P, 1], F32, "warm")
        nc.vector.memset(warm[:], 0.0)
        nc.scalar.activation(warm[:], warm[:], ACT.Silu)

        lists = [kept([P, S // PER_COLUMN], U16, "list%d" % i) for i in range(3)]
        nc.sync.dma_start(lists[0][:], offs)
        nc.sync.dma_start(lists[1][:], offs2)
        table = [kept([P, T], I32, "table%d" % a) for a in range(PASSES)]
        raw = {}

        def load_weight(side, a, first, width, tag):
            piece = ring.tile([P, PACK, width], F32, name=tag, align_bytes=64, bufs=1 if tag == "raw_wb" else 2)
            rows = (wa, wb)[side][a * K_PASS : (a + 1) * K_PASS, first : first + width]
            nc.sync.dma_start(piece[:], rows.rearrange("(p j) c -> p j c", j=PACK))
            raw.setdefault((side, a), []).append(piece)

        def load_table(a):
            nc.sync.dma_start(table[a][:], tab_words[a].rearrange("p n t -> p (n t)").bitcast(I32))

        w4_raw = kept([P, PASSES, 2 * H], U8, "w4_raw")
        nc.sync.dma_start(w4_raw[:].bitcast(I32), w4_words.rearrange("a p c -> p a c").bitcast(I32))
        for q in range(QUADRANTS):
            nc.sync.dma_start(
                tab_plane[32 * q : 32 * q + 4 * PASSES, :].bitcast(I32),
                tab_scales[:, 4 * q : 4 * q + 4, :].bitcast(I32))
        load_weight(0, 0, 0, H, "raw_wa")
        load_table(0)
        load_table(1)
        load_weight(0, 1, 0, H, "raw_wa")
        load_weight(1, 0, 0, H, "raw_wb")
        load_weight(1, 1, 0, H // 2, "raw_half")
        load_weight(1, 1, H // 2, H // 2, "raw_half")
        for q in range(QUADRANTS):
            nc.sync.dma_start(
                w4_plane_raw[32 * q : 32 * q + 4, :, :].bitcast(I32),
                w4_scales[:, 4 * q : 4 * q + 4, :].rearrange("a r c -> r a c").bitcast(I32))
        gains = kept([P, PACK], F32, "gains")
        nc.sync.dma_start(gains[:], gain.rearrange("(p t) -> p t", t=PACK))
        w8_codes = kept([P, N], I32, "w8_codes")
        nc.sync.dma_start(w8_codes[:], w8_words[0].rearrange("p n t -> p (n t)").bitcast(I32))
        for q in range(QUADRANTS):
            nc.sync.dma_start(
                w8_plane[32 * q : 32 * q + 4, :].bitcast(I32), w8_scales[0, 4 * q : 4 * q + 4, :].bitcast(I32))

        pages = [kept([P, T2], F32, "page%d" % b) for b in range(PAGES)]
        for page in pages:
            nc.gpsimd.memset(page[:], 0.0)

        codes = {}
        scales = {}

        def quantise_weight(side, a):
            rounded = ring.tile([P, PACK * H], BF16, name="rounded", align_bytes=64)
            dealt = rounded[:].rearrange("p (t m j) -> p m t j", t=PACK, j=PACK)
            share = P // len(raw[side, a])
            for i, piece in enumerate(raw[side, a]):
                (nc.vector.tensor_copy if (side, a, i) in ((1, 1, 1),) else nc.scalar.copy)(
                    dealt[:, share * i : share * (i + 1)], piece[:].rearrange("p j (m t) -> p m t j", t=PACK))
            codes[side, a] = kept([P, H], U32, "codes%d_%d" % (side, a))
            scales[side, a] = kept([P, H], U8, "scales%d_%d" % (side, a))
            nc.vector.quantize_mx(codes[side, a][:].bitcast(FP8X4), scales[side, a][:], rounded[:])

        planes = [kept([P, S], U8, "plane%d" % side) for side in range(2)]
        for side in range(2):
            nc.vector.tensor_copy(planes[side][:], tab_plane[:].indirect(lists[side][:]))
        for a in range(PASSES):
            quantise_weight(0, a)
        for q in range(QUADRANTS):
            nc.sync.dma_start(
                second_pass_plane[32 * q : 32 * q + 4, :].bitcast(I32),
                planes[0][32 * q + 4 : 32 * q + 8, :].bitcast(I32))

        winds = [
            ring.tile([P, BLOCKS, GROUP], F32, name="raw_wa", align_bytes=64) if g < PASSES
            else kept([P, BLOCKS, GROUP], F32, "wind%d" % g)
            for g in range(GROUPS)]
        factors = kept([P, S], F32, "factors")
        wind_rows = wind.rearrange("(b p) s -> p b s", p=P)
        nc.sync.dma_start(winds[0][:], wind_rows[:, :, 0:GROUP])
        nc.sync.dma_start(lists[2][:], offs3)
        nc.sync.dma_start(factors[:], wgo)
        for g in range(1, GROUPS):
            nc.sync.dma_start(winds[g][:], wind_rows[:, :, g * GROUP : (g + 1) * GROUP])

        words = {}
        for a in range(PASSES):
            for side in range(2):
                words[side, a] = kept([P, S], U32, "words%d_%d" % (side, a))
                nc.vector.tensor_copy(words[side, a][:], table[a][:].bitcast(U32).indirect(lists[side][:]))
        for a in range(PASSES):
            quantise_weight(1, a)

        w4_codes = kept([P, PASSES, 2 * H], U8, "w4_codes")
        nc.vector.tensor_copy(
            w4_codes[:].bitcast(U16).rearrange("p a (t m) -> p a t m", t=PACK),
            w4_raw[:].bitcast(U16).rearrange("p a (m t) -> p a t m", t=PACK))
        w4_plane = kept([P, PASSES, H], U8, "w4_plane")
        nc.vector.tensor_copy(
            w4_plane[:].rearrange("p a (t m) -> p a t m", t=PACK),
            w4_plane_raw[:].rearrange("p a (m t) -> p a t m", t=PACK))

        waves = {}
        quantised_h = {}
        scores = kept([P, BLOCKS, S], F32, "scores")

        def group_words(side, a, g, first, count):
            return words[side, a][:, g * GROUP + first : g * GROUP + first + count].bitcast(FP8X4)

        def wave(side, g):
            entries = slice(g * GROUP, (g + 1) * GROUP)
            waves[side, g] = ring.tile([P, PACK, GROUP], F32, name="wave%d" % side, bufs=3 - side)
            shifted = ring.tile([P, PACK, GROUP], U32, name="shifted")
            pairs = (slice(0, 2), slice(2, 4))
            for pair in pairs:
                bank = psum.tile([P, 2, GROUP], F32, name="angle", bufs=3)
                for i in range(2):
                    run = slice((pair.start + i) * P, (pair.start + i + 1) * P)
                    for a in range(PASSES):
                        nc.tensor.matmul_mx(
                            bank[:, i, :],
                            lhsT=codes[side, a][:, run].bitcast(FP8X4), lhsT_scale=scales[side, a][:, run],
                            rhs=group_words(side, a, g, 0, GROUP), rhs_scale=planes[side][4 * a : P, entries],
                            start=(a == 0), stop=(a == PASSES - 1))
                nc.scalar.activation(waves[side, g][:, pair], bank[:], ACT.Copy, bias=0.25 * side, scale=1.0 / TURN)
            for pair in pairs:
                if (side, g) in ((0, 0), (1, 0)):
                    nc.vector.tensor_scalar(shifted[:, pair].bitcast(I32), waves[side, g][:, pair], ROUNDER, None, ALU.add)
                else:
                    nc.scalar.activation(shifted[:, pair], waves[side, g][:, pair], ACT.Copy, bias=ROUNDER, scale=1.0)
            for pair in pairs:
                nc.vector.scalar_tensor_tensor(
                    waves[side, g][:, pair], shifted[:, pair].bitcast(I32), ROUNDER, waves[side, g][:, pair],
                    ALU.subtract, ALU.subtract)
            for pair in pairs:
                nc.scalar.activation(waves[side, g][:, pair], waves[side, g][:, pair], ACT.Sin, scale=-TURN)

        def make_h(g):
            product = waves[0, g]
            for t in range(PACK):
                nc.vector.scalar_tensor_tensor(
                    product[:, t], waves[0, g][:, t], gains[:, t : t + 1], waves[1, g][:, t], ALU.mult, ALU.mult)
            h = ring.tile([P, GROUP * PACK], BF16, name="h", align_bytes=64)
            for first in range(0, GROUP, P):
                own = psum.tile([P, PACK, P], F32, name="own")
                entries = slice(g * GROUP + first, g * GROUP + first + P)
                for t in range(PACK):
                    for a in range(PASSES):
                        nc.tensor.matmul_mx(
                            own[:, t, :],
                            lhsT=w4_codes[:, a, 2 * t * P : 2 * (t + 1) * P].bitcast(FP4X4),
                            lhsT_scale=w4_plane[:, a, t * P : (t + 1) * P],
                            rhs=group_words(0, a, g, first, P),
                            rhs_scale=(planes[0], second_pass_plane)[a][:, entries],
                            start=(a == 0), stop=(a == PASSES - 1))
                nc.vector.tensor_tensor(
                    h[:, first * PACK : (first + P) * PACK].rearrange("p (n i t) -> p n t i", i=2, t=PACK),
                    product[:, :, first : first + P].rearrange("p t (n i) -> p n t i", i=2),
                    own[:].rearrange("p t (n i) -> p n t i", i=2),
                    ALU.add)
            h_codes = ring.tile([P, GROUP], U32, name="h_codes", align_bytes=64)
            h_scales = ring.tile([P, GROUP], U8, name="h_scales", align_bytes=64)
            nc.vector.quantize_mx(h_codes[:].bitcast(FP8X4), h_scales[:], h[:])
            quantised_h[g] = (h_codes, h_scales)

        def score(g, first_block, tag):
            h_codes, h_scales = quantised_h[g]
            blocks = slice(first_block, first_block + 2)
            bank = psum.tile([P, 2, GROUP], F32, name=tag, bufs=3)
            for i in range(2):
                rows = slice((first_block + i) * P, (first_block + i + 1) * P)
                nc.tensor.matmul_mx(
                    bank[:, i, :],
                    lhsT=w8_codes[:, rows].bitcast(FP8X4), lhsT_scale=w8_plane[:, rows],
                    rhs=h_codes[:].bitcast(FP8X4), rhs_scale=h_scales[:],
                    start=True, stop=True)
            nc.vector.tensor_tensor(
                scores[:, blocks, g * GROUP : (g + 1) * GROUP], bank[:], winds[g][:, blocks, :], ALU.mult)

        def place(b, first, count):
            nc.vector.tensor_tensor(
                pages[b % PAGES][:].indirect(lists[2][:, list_columns(first, count)]),
                scores[:, b, first : first + count], factors[:, first : first + count], ALU.mult)
            if first + count == S:
                nc.sync.dma_start(out[b * P : (b + 1) * P, :], pages[b % PAGES][:])

        def bound_and_place(b, first, count):
            part = scores[:, b, first : first + count]
            nc.scalar.activation(part, part, ACT.Tanh)
            place(b, first, count)

        for g in range(GROUPS):
            wave(0, g)
            wave(1, g)
            make_h(g)
            for b in range(0, BLOCKS, 2):
                score(g, b, "score")
            for b, first, count in {1: [(0, 0, 512), (1, 0, 512)], 3: [(0, 512, 512), (1, 512, 512)]}.get(g, ()):
                bound_and_place(b, first, count)
        for b in range(EARLY, BLOCKS):
            bound_and_place(b, 0, S)
